import numpy as np
import ml_dtypes


def mxq(x, axis, fmt="e4m3"):
    dtype, down = {"e4m3": (ml_dtypes.float8_e4m3fn, 7), "e5m2": (ml_dtypes.float8_e5m2, 14)}[fmt]
    v = np.moveaxis(np.asarray(x, np.float32).astype(ml_dtypes.bfloat16).astype(np.float64), axis, -1)
    blocks = v.reshape(v.shape[:-1] + (-1, 32))
    amax = np.abs(blocks).max(-1, keepdims=True)
    byte = np.maximum(np.where(amax > 0, np.frexp(amax)[1] - 1 + 127, 0) - down, 1)
    scale = np.exp2(byte - 127.0)
    codes = (blocks / scale).astype(np.float32).astype(dtype).astype(np.float64)
    return np.moveaxis((codes * scale).reshape(v.shape), -1, axis)


WIDE = False


def mx_kscale(k):
    if not WIDE:
        return np.ones(k)
    levels = np.array([10, -10, 5, -5, 0])
    if k % 512:
        return np.exp2(np.random.permutation(np.resize(levels, k // 32))).repeat(32)
    a = np.empty((k // 512, 16))
    for p in range(k // 512):
        a[p, :8] = np.random.permutation(np.resize(levels, 8))
        for g in range(8):
            far = levels[np.abs(levels - a[p, g]) >= 10]
            a[p, g + 8] = far[np.random.randint(len(far))]
    return np.exp2(a.ravel()).repeat(32)


BF16 = ml_dtypes.bfloat16


def bf(x):
    return np.asarray(x, np.float32).astype(BF16)


def f64(x):
    return np.asarray(x).astype(np.float64)


E2M1 = np.array([0.0, 0.5, 1.0, 1.5, 2.0, 3.0, 4.0, 6.0, -0.0, -0.5, -1.0, -1.5, -2.0, -3.0, -4.0, -6.0])


def pack_weight(w, fmt):
    k, n = w.shape
    w = f64(bf(w)).reshape(k // 32, 32, n)
    amax = np.abs(w).max(1)
    if fmt == "e4m3":
        byte = np.frexp(amax)[1] - 1 + 127 - 7
    else:
        mant, ex = np.frexp(amax / 6.0)
        byte = np.where(mant > 0.5, ex, ex - 1) + 127
    byte = np.clip(np.where(amax > 0, byte, 1), 1, 254)
    scaled = (w * np.exp2(127.0 - byte)[:, None, :]).reshape(k, n).astype(np.float32)
    by_word = np.ascontiguousarray(scaled.reshape(k // 512, 128, 4, n).transpose(0, 1, 3, 2))
    if fmt == "e4m3":
        words = by_word.astype(ml_dtypes.float8_e4m3fn).view(np.uint8)
    else:
        c = by_word.astype(ml_dtypes.float4_e2m1fn).view(np.uint8) & 0xF
        words = c[..., 0::2] | (c[..., 1::2] << 4)
    return np.ascontiguousarray(words), np.ascontiguousarray(byte.astype(np.uint8).reshape(k // 512, 16, n))


def unpack_weight(words, scales, fmt):
    g, p, n, _ = words.shape
    if fmt == "e4m3":
        vals = np.ascontiguousarray(words).view(ml_dtypes.float8_e4m3fn).astype(np.float64)
    else:
        nib = np.empty((g, p, n, 4), np.uint8)
        nib[..., 0::2] = words & 0xF
        nib[..., 1::2] = words >> 4
        vals = E2M1[nib]
    vals = vals * np.repeat(np.exp2(scales.astype(np.float64) - 127.0), 8, axis=1)[..., None]
    return vals.transpose(0, 1, 3, 2).reshape(g * 512, n)
def pack4(w):
    words, scales = pack_weight(w, "e2m1")
    return words.reshape(words.shape[0], 128, -1), scales


def unpack4(words, scales):
    return unpack_weight(words.reshape(words.shape[0], 128, -1, 2), scales, "e2m1")


def planes(Y):
    n, m = Y.shape
    b = f64(bf(Y)).reshape(n // 32, 32, m)
    amax = np.abs(b).max(1)
    byte = np.clip(np.where(amax > 0, np.frexp(amax)[1] - 1 + 127 - 7, 1), 1, 254)
    codes = (b * np.exp2(127.0 - byte)[:, None, :]).reshape(n, m).astype(np.float32).astype(ml_dtypes.float8_e4m3fn).view(np.uint8)
    words = codes.reshape(n // 512, 128, 4, m).transpose(0, 1, 3, 2)
    return np.ascontiguousarray(words), np.ascontiguousarray(byte.astype(np.uint8).reshape(n // 512, 16, m))


U, D, C, I, P = 1024, 512, 1024, 2048, 512

def sig(x):
    return 1.0 / (1.0 + np.exp(-x))

def setup_inputs():
    s_d, s_c, t = mx_kscale(D), mx_kscale(C), mx_kscale(I)
    user_emb = bf(np.random.randn(U, D) * s_d)
    item_emb = bf(0.8 / np.sqrt(D) * np.random.randn(I, D) / s_d)
    user_content = bf(np.random.randn(U, C) * s_c)
    item_content_words, item_content_scales = pack4(0.7 / np.sqrt(C) * np.random.randn(C, I) / s_c[:, None])
    ref_score = bf(0.4 * np.random.randn(I))
    pop_gate = bf(sig(np.random.randn(I)) * t)
    mix_words, mix_scales = pack_weight(2.0 / np.sqrt(I) * np.random.randn(I, P) / t[:, None], "e4m3")
    cell_bias = bf(0.4 * np.random.randn(P))
    cell_gain = bf(np.exp(0.8 * np.random.randn(P)))
    user_gate = bf(sig(1.0 + np.random.randn(U)))
    return dict(user_emb=user_emb, item_emb=item_emb, user_content=user_content,
                item_content_words=item_content_words, item_content_scales=item_content_scales,
                ref_score=ref_score, pop_gate=pop_gate, mix_words=mix_words, mix_scales=mix_scales,
                cell_bias=cell_bias, cell_gain=cell_gain, user_gate=user_gate)

def reference(user_emb, item_emb, user_content, item_content_words, item_content_scales,
              ref_score, pop_gate, mix_words, mix_scales, cell_bias, cell_gain, user_gate):
    ue = mxq(f64(user_emb), 1, "e4m3")
    ie = mxq(f64(item_emb), 1, "e4m3")
    uc = mxq(f64(user_content), 1, "e4m3")
    ic = unpack4(item_content_words, item_content_scales)
    S = (ue @ ie.T) + (uc @ ic)
    H = (S - f64(ref_score)) * f64(pop_gate)
    hq = mxq(H, 1, "e4m3")
    mix = unpack_weight(mix_words, mix_scales, "e4m3")
    Z = hq @ mix
    y = (Z + f64(cell_bias)) * f64(cell_gain) * f64(user_gate)[:, None]
    Y = y.T
    words, scales = planes(Y)
    return y, words, scales

@@ -1,0 +1,401 @@
+from contextlib import ExitStack
+
+import concourse.mybir as mybir
+from concourse.masks import make_identity
+
+U, D, C, I, P = 1024, 512, 1024, 2048, 512
+FLOPS = 2 * U * I * (D + C) + 2 * U * I * P
+
+F32 = mybir.dt.float32
+BF16 = mybir.dt.bfloat16
+U32 = mybir.dt.uint32
+I32 = mybir.dt.int32
+U8 = mybir.dt.uint8
+FP8X4 = mybir.dt.float8_e4m3fn_x4
+FP4X4 = mybir.dt.float4_e2m1fn_x4
+ALU = mybir.AluOpType
+ACT = mybir.ActivationFunctionType
+
+PARTS = 128
+PACK = 4
+SPAN = 512
+BANKS = 8
+
+
+def tile_popularity_gated_slate_exposure_k6_kernel(
+    tc, user_emb, item_emb, user_content, item_content_words, item_content_scales, ref_score, pop_gate,
+    mix_words, mix_scales, cell_bias, cell_gain, user_gate, out_0, out_1, out_2,
+):
+    nc = tc.nc
+    with ExitStack() as ctx:
+        keep = ctx.enter_context(tc.tile_pool(name="keep", bufs=1))
+        stage = ctx.enter_context(tc.tile_pool(name="stage", bufs=3))
+        psum = ctx.enter_context(tc.psum_pool(name="psum", bufs=1))
+        ctx.enter_context(tc.manual_schedule())
+
+        banks_used = []
+
+        def next_bank(dtype=F32, width=SPAN):
+            name = "bank%d" % (len(banks_used) % BANKS)
+            banks_used.append(name)
+            return psum.tile([PARTS, width], dtype, name=name)
+
+        def kept(name, shape, dtype):
+            return keep.tile(shape, dtype, name=name, align_bytes=64)
+
+        ue_raw = [kept("ue_raw%d" % b, [PARTS, 2, D], BF16) for b in range(4)]
+        uc_raw = [kept("uc_raw%d" % b, [PARTS, 2, C], BF16) for b in range(4)]
+        ie_raw = [kept("ie_raw%d" % g, [PARTS, PACK, D], BF16) for g in range(4)]
+        b_words_raw = [kept("b_words_raw%d" % g, [PARTS, 2, 2 * SPAN], U8) for g in range(4)]
+        b_scales_raw = kept("b_scales_raw", [PARTS, 2, I], U8)
+        b_words = [kept("b_words%d" % g, [PARTS, 2, PACK, 2 * PARTS], U8) for g in range(4)]
+        b_scales = [kept("b_scales%d" % g, [PARTS, 2, PACK, PARTS], U8) for g in range(4)]
+        x_words_raw = kept("x_words_raw", [PARTS, 4, P], U32)
+        x_scales_raw = kept("x_scales_raw", [PARTS, P], U8)
+        x_words = kept("x_words", [PARTS, 4, P], U32)
+        x_scales = kept("x_scales", [PARTS, P], U8)
+        ref_raw = kept("ref_raw", [PARTS, 4, PACK], BF16)
+        pop_raw = kept("pop_raw", [PARTS, 4, PACK], BF16)
+        pop = kept("pop", [PARTS, 4, PACK], F32)
+        neg_ref_pop = kept("neg_ref_pop", [PARTS, 4, PACK], F32)
+        bias_raw = kept("bias_raw", [PARTS, PACK], BF16)
+        gain_raw = kept("gain_raw", [PARTS, PACK], BF16)
+        gain = kept("gain", [PARTS, PACK], F32)
+        bias_gain = kept("bias_gain", [PARTS, PACK], F32)
+        gate_rows = kept("gate_rows", [PARTS, PARTS], BF16)
+        gate_cols = kept("gate_cols", [PARTS, 8], F32)
+        gate_wide = kept("gate_wide", [PARTS, U], BF16)
+        ident = kept("ident", [PARTS, PARTS], F32)
+        ident_bf = kept("ident_bf", [PARTS, PARTS], BF16)
+        y_codes = kept("y_codes", [PARTS, U], U32)
+        y_scales = kept("y_scales", [PARTS, U], U8)
+        quantised = {}
+        grouped = {}
+        h_rows = {}
+        w_rows = {}
+        z_banks = {}
+
+        def load_users(src, dst, b):
+            nc.sync.dma_start(out=dst[b][:], in_=src[256 * b : 256 * b + 256, :].rearrange("(p j) k -> p j k", j=2))
+
+        def load_items(g):
+            nc.sync.dma_start(out=ie_raw[g][:], in_=item_emb[SPAN * g : SPAN * (g + 1), :].rearrange("(m t) k -> m t k", t=PACK))
+
+        def load_b_words(g):
+            src = item_content_words[:, :, 2 * SPAN * g : 2 * SPAN * (g + 1)].rearrange("c p n -> p c n")
+            nc.sync.dma_start(out=b_words_raw[g][:].bitcast(I32), in_=src.bitcast(I32))
+
+        nc.vector.memset(b_scales_raw[:].bitcast(I32), 0)
+        nc.vector.memset(x_scales_raw[:].bitcast(I32), 0)
+        make_identity(nc, ident[:])
+        nc.gpsimd.memset(gate_rows[:], 0.0)
+        make_identity(nc, ident_bf[:])
+
+        load_users(user_emb, ue_raw, 0)
+        load_users(user_emb, ue_raw, 1)
+        load_items(0)
+        load_b_words(0)
+        load_users(user_content, uc_raw, 0)
+        load_users(user_content, uc_raw, 1)
+        for q in range(4):
+            src = item_content_scales[:, 4 * q : 4 * q + 4, :].rearrange("c r n -> r c n")
+            nc.sync.dma_start(out=b_scales_raw[32 * q : 32 * q + 4, :, :].bitcast(I32), in_=src.bitcast(I32))
+        nc.sync.dma_start(out=ref_raw[:], in_=ref_score.rearrange("(g p t) -> p g t", g=4, t=PACK))
+        nc.sync.dma_start(out=pop_raw[:], in_=pop_gate.rearrange("(g p t) -> p g t", g=4, t=PACK))
+        for g in range(1, 4):
+            load_items(g)
+            load_b_words(g)
+        for b in (2, 3):
+            load_users(user_emb, ue_raw, b)
+        for b in (2, 3):
+            load_users(user_content, uc_raw, b)
+        nc.sync.dma_start(out=x_words_raw[:].bitcast(I32), in_=mix_words.rearrange("g p n t -> p g (n t)").bitcast(I32))
+        for q in range(4):
+            nc.sync.dma_start(
+                out=x_scales_raw[32 * q : 32 * q + 16, :].bitcast(I32),
+                in_=mix_scales[:, 4 * q : 4 * q + 4, :].bitcast(I32),
+            )
+        nc.sync.dma_start(out=bias_raw[:], in_=cell_bias.rearrange("(p t) -> p t", t=PACK))
+        nc.sync.dma_start(out=gain_raw[:], in_=cell_gain.rearrange("(p t) -> p t", t=PACK))
+        nc.sync.dma_start(out=gate_rows[0:8, :], in_=user_gate.rearrange("(j p) -> j p", p=PARTS))
+        nc.sync.dma_start(out=gate_wide[:], in_=user_gate.partition_broadcast(PARTS))
+
+        def copy_on(engine, out, in_):
+            if engine == "scalar":
+                nc.scalar.copy(out=out, in_=in_)
+            else:
+                nc.vector.tensor_copy(out=out, in_=in_)
+
+        def turn(key, part, engine):
+            kind = key[0]
+            if kind == "ie":
+                words, rows, first = ie_raw[key[1]][:].bitcast(F32), (2 * part, 2 * part + 1), 0
+            elif kind == "ue":
+                words, rows, first = ue_raw[2 * key[1] + part][:].bitcast(F32), (0, 1), 0
+            else:
+                words, rows, first = uc_raw[2 * key[1] + part][:].bitcast(F32), (0, 1), 256 * key[2]
+            bank = next_bank()
+            for j, row in enumerate(rows):
+                for u in range(2):
+                    col = (2 * j + u) * PARTS
+                    nc.tensor.transpose(bank[:, col : col + PARTS], words[:, row, first + u : first + 256 : 2], ident[:])
+            if key not in grouped:
+                grouped[key] = stage.tile([PARTS, PACK * SPAN], BF16, name="grouped", align_bytes=64, bufs=4)
+            dst = grouped[key][:].bitcast(F32)[:, SPAN * part : SPAN * (part + 1)]
+            if kind == "ie":
+                copy_on(engine, dst.rearrange("p (j r u) -> p j r u", j=2, u=2), bank[:].rearrange("p (j u r) -> p j r u", j=2, u=2))
+            else:
+                copy_on(engine, dst.rearrange("p (r j u) -> p r j u", j=2, u=2), bank[:].rearrange("p (j u r) -> p r j u", j=2, u=2))
+
+        def quantise(key, first=0, width=SPAN):
+            if key not in quantised:
+                name = "_".join(str(k) for k in key)
+                quantised[key] = (kept("codes_" + name, [PARTS, SPAN], U32), kept("scales_" + name, [PARTS, SPAN], U8))
+            codes, scales = quantised[key]
+            nc.vector.quantize_mx(
+                out=codes[:, first : first + width].bitcast(FP8X4), scales=scales[:, first : first + width],
+                in_=grouped[key][:, PACK * first : PACK * (first + width)],
+            )
+
+        def order_b_words(g):
+            nc.vector.tensor_copy(
+                out=b_words[g][:].rearrange("p c t (m b) -> p c t m b", b=2),
+                in_=b_words_raw[g][:].rearrange("p c (m t b) -> p c t m b", t=PACK, b=2),
+            )
+
+        def order_b_scales(g):
+            nc.vector.tensor_copy(
+                out=b_scales[g][:],
+                in_=b_scales_raw[:, :, SPAN * g : SPAN * (g + 1)].rearrange("p c (m t) -> p c t m", t=PACK),
+            )
+
+        def order_x():
+            nc.vector.tensor_copy(
+                out=x_words[:].bitcast(I32).rearrange("p g (t c i) -> p g c t i", t=PACK, i=4),
+                in_=x_words_raw[:].bitcast(I32).rearrange("p g (c i t) -> p g c t i", t=PACK, i=4),
+            )
+            nc.vector.tensor_copy(
+                out=x_scales[:].rearrange("p (t m) -> p t m", t=PACK),
+                in_=x_scales_raw[:].rearrange("p (m t) -> p t m", t=PACK),
+            )
+
+        s_banks = {}
+
+        def score_pass(h, g, t, c, start, stop):
+            if start:
+                s_banks[h, g, t] = next_bank()
+            cols = slice(PARTS * t, PARTS * (t + 1))
+            if c == "emb":
+                codes, scales = quantised["ie", g]
+                lhs, lhs_scale = codes[:, cols].bitcast(FP8X4), scales[:, cols]
+                rhs, rhs_scale = quantised["ue", h]
+            else:
+                lhs, lhs_scale = b_words[g][:, c, t, :].bitcast(FP4X4), b_scales[g][:, c, t, :]
+                rhs, rhs_scale = quantised["uc", h, c]
+            nc.tensor.matmul_mx(
+                out=s_banks[h, g, t][:], lhsT=lhs, lhsT_scale=lhs_scale,
+                rhs=rhs[:].bitcast(FP8X4), rhs_scale=rhs_scale[:], start=start, stop=stop,
+            )
+
+        def gate_scores(h, g, t):
+            if t == 0:
+                h_rows[h, g] = stage.tile([PARTS, PACK, SPAN], BF16, name="h_rows", align_bytes=64)
+            nc.scalar.activation(
+                out=h_rows[h, g][:, t, :], in_=s_banks[h, g, t][:], func=ACT.Identity,
+                bias=neg_ref_pop[:, g, t : t + 1], scale=pop[:, g, t : t + 1],
+            )
+
+        def scores(h, g):
+            for t in range(PACK):
+                score_pass(h, g, t, "emb", True, False)
+                score_pass(h, g, t, 0, False, False)
+                score_pass(h, g, t, 1, False, True)
+                gate_scores(h, g, t)
+
+        def interleave_h(h, g, engine="vector", first=0, width=SPAN):
+            if first == 0:
+                grouped["h", h, g] = stage.tile([PARTS, PACK * SPAN], BF16, name="grouped", align_bytes=64, bufs=4)
+            copy_on(
+                engine,
+                grouped["h", h, g][:, PACK * first : PACK * (first + width)].rearrange("p (c i t) -> p c t i", t=PACK, i=4),
+                h_rows[h, g][:, :, first : first + width].rearrange("p t (c i) -> p c t i", i=4),
+            )
+
+        def mix_pass(first, width, t, g):
+            if g == 0:
+                z_banks[first, t] = next_bank(F32, width)
+            cols = slice(PARTS * t, PARTS * (t + 1))
+            codes, scales = quantised["h", first // SPAN, g]
+            users = slice(first % SPAN, first % SPAN + width)
+            nc.tensor.matmul_mx(
+                out=z_banks[first, t][:], lhsT=x_words[:, g, cols].bitcast(FP8X4), lhsT_scale=x_scales[4 * g : PARTS, cols],
+                rhs=codes[:, users].bitcast(FP8X4), rhs_scale=scales[:, users], start=(g == 0), stop=(g == 3),
+            )
+
+        def scale_on(engine, out, in_, scale, bias):
+            if engine == "scalar":
+                nc.scalar.activation(out=out, in_=in_, func=ACT.Identity, bias=bias, scale=scale)
+            else:
+                nc.vector.tensor_scalar(out=out, in0=in_, scalar1=scale, scalar2=bias, op0=ALU.mult, op1=ALU.add)
+
+        def cell_affine(first, width, t, engine):
+            if t == 0:
+                w_rows[first] = kept("w_rows%d" % first, [PARTS, PACK, width], F32)
+            scale_on(engine, w_rows[first][:, t, :], z_banks[first, t][:], gain[:, t : t + 1], bias_gain[:, t : t + 1])
+
+        def turn_out(first, j, engine="scalar"):
+            bank = next_bank()
+            for t in range(PACK):
+                nc.tensor.transpose(bank[:, PARTS * t : PARTS * (t + 1)], w_rows[first][:, t, PARTS * j : PARTS * (j + 1)], ident[:])
+            y_rows = stage.tile([PARTS, P], F32, name="y_rows", bufs=4)
+            tile_no = first // PARTS + j
+            out = y_rows[:].rearrange("u (p t) -> u p t", t=PACK)
+            in_ = bank[:].rearrange("u (t p) -> u p t", t=PACK)
+            gate = gate_cols[:, tile_no : tile_no + 1]
+            if engine == "scalar":
+                nc.scalar.activation(out=out, in_=in_, func=ACT.Copy, scale=gate)
+            else:
+                nc.vector.tensor_scalar(out=out, in0=in_, scalar1=gate, scalar2=None, op0=ALU.mult)
+            nc.sync.dma_start(out=out_0[PARTS * tile_no : PARTS * (tile_no + 1), :], in_=y_rows[:])
+
+        def gate_y(first, width):
+            grouped["y", first] = stage.tile([PARTS, PACK * width], BF16, name="y_grouped", align_bytes=64)
+            nc.vector.tensor_tensor(
+                out=grouped["y", first][:].rearrange("p (c i t) -> p c t i", t=PACK, i=4),
+                in0=w_rows[first][:].rearrange("p t (c i) -> p c t i", i=4),
+                in1=gate_wide[:, first : first + width].rearrange("p (c i) -> p c i", i=4).unsqueeze(2).to_broadcast([PARTS, width // 4, PACK, 4]),
+                op=ALU.mult,
+            )
+
+        def quantise_y(first, width):
+            cols = slice(first, first + width)
+            nc.vector.quantize_mx(out=y_codes[:, cols].bitcast(FP8X4), scales=y_scales[:, cols], in_=grouped["y", first][:])
+
+        def store_codes(first, width):
+            cols = slice(first, first + width)
+            nc.sync.dma_start(out=out_1[0].rearrange("p m t -> p (m t)").bitcast(I32)[:, cols], in_=y_codes[:, cols].bitcast(I32))
+
+        def store_scales():
+            for q in range(4):
+                nc.sync.dma_start(out=out_2[0, 4 * q : 4 * q + 4, :].bitcast(I32), in_=y_scales[32 * q : 32 * q + 4, :].bitcast(I32))
+
+        def item_constants():
+            nc.vector.tensor_copy(out=pop[:], in_=pop_raw[:])
+            nc.vector.scalar_tensor_tensor(out=neg_ref_pop[:], in0=ref_raw[:], scalar=-1.0, in1=pop_raw[:], op0=ALU.mult, op1=ALU.mult)
+
+        def cell_constants():
+            nc.vector.tensor_copy(out=gain[:], in_=gain_raw[:])
+            nc.vector.tensor_tensor(out=bias_gain[:], in0=bias_raw[:], in1=gain_raw[:], op=ALU.mult)
+
+        def user_constants():
+            bank = next_bank(BF16, PARTS)
+            nc.tensor.transpose(bank[:], gate_rows[:], ident_bf[:])
+            nc.vector.tensor_copy(out=gate_cols[:], in_=bank[:, 0:8])
+
+        turn(("ue", 0), 0, "scalar")
+        turn(("ue", 0), 1, "vector")
+        turn(("ie", 0), 0, "scalar")
+        quantise(("ue", 0))
+        turn(("ie", 0), 1, "scalar")
+        order_b_words(0)
+        quantise(("ie", 0))
+        turn(("uc", 0, 0), 0, "scalar")
+        turn(("uc", 0, 1), 0, "scalar")
+        turn(("uc", 0, 0), 1, "scalar")
+        turn(("uc", 0, 1), 1, "vector")
+        quantise(("uc", 0, 0))
+        order_b_scales(0)
+        quantise(("uc", 0, 1))
+        item_constants()
+        for t in range(PACK):
+            score_pass(0, 0, t, "emb", True, False)
+        turn(("ie", 1), 0, "scalar")
+        turn(("ie", 1), 1, "scalar")
+        order_b_words(1)
+        quantise(("ie", 1))
+        order_b_scales(1)
+        for t in range(PACK):
+            score_pass(0, 0, t, 0, False, False)
+            score_pass(0, 0, t, 1, False, True)
+            gate_scores(0, 0, t)
+        turn(("ie", 2), 0, "scalar")
+        turn(("ie", 2), 1, "scalar")
+        interleave_h(0, 0)
+        order_b_words(2)
+        quantise(("ie", 2))
+        order_b_scales(2)
+        quantise(("h", 0, 0))
+        scores(0, 1)
+        turn(("ie", 3), 0, "scalar")
+        turn(("ie", 3), 1, "scalar")
+        turn(("ue", 1), 0, "scalar")
+        turn(("ue", 1), 1, "scalar")
+        order_b_words(3)
+        interleave_h(0, 1)
+        quantise(("ie", 3))
+        order_b_scales(3)
+        quantise(("h", 0, 1))
+        quantise(("ue", 1))
+        scores(0, 2)
+        turn(("uc", 1, 0), 0, "scalar")
+        turn(("uc", 1, 0), 1, "vector")
+        turn(("uc", 1, 1), 0, "scalar")
+        turn(("uc", 1, 1), 1, "vector")
+        interleave_h(0, 2)
+        quantise(("uc", 1, 0))
+        quantise(("uc", 1, 1))
+        quantise(("h", 0, 2))
+        scores(0, 3)
+        interleave_h(0, 3)
+        cell_constants()
+        quantise(("h", 0, 3))
+        scores(1, 0)
+        order_x()
+        interleave_h(1, 0)
+        user_constants()
+        quantise(("h", 1, 0))
+        scores(1, 1)
+        interleave_h(1, 1)
+        for t in range(PACK):
+            for g in range(4):
+                mix_pass(0, SPAN, t, g)
+            cell_affine(0, SPAN, t, "scalar")
+        quantise(("h", 1, 1))
+        scores(1, 2)
+        gate_y(0, SPAN)
+        interleave_h(1, 2)
+        quantise_y(0, SPAN)
+        store_codes(0, SPAN)
+        for j in range(4):
+            turn_out(0, j)
+        quantise(("h", 1, 2))
+        scores(1, 3)
+        interleave_h(1, 3, "vector", 0, 256)
+        interleave_h(1, 3, "scalar", 256, 256)
+        quantise(("h", 1, 3), 0, 256)
+        quantise(("h", 1, 3), 256, 256)
+        for g in range(3):
+            for t in range(PACK):
+                mix_pass(512, 256, t, g)
+        for t in (0, 1):
+            for g in range(3):
+                mix_pass(768, 256, t, g)
+        for t in range(PACK):
+            mix_pass(512, 256, t, 3)
+            cell_affine(512, 256, t, "scalar" if t in (0, 2) else "vector")
+        gate_y(512, 256)
+        for t in (2, 3):
+            for g in range(3):
+                mix_pass(768, 256, t, g)
+        for t in range(PACK):
+            mix_pass(768, 256, t, 3)
+            cell_affine(768, 256, t, "scalar" if t in (0, 1, 2) else "vector")
+        quantise_y(512, 256)
+        turn_out(512, 0, "scalar")
+        turn_out(512, 1, "scalar")
+        gate_y(768, 256)
+        turn_out(768, 0, "scalar")
+        quantise_y(768, 256)
+        store_codes(512, 512)
+        turn_out(768, 1, "scalar")
+        store_scales()

@@ -3,8 +3,8 @@ from contextlib import ExitStack
 import concourse.mybir as mybir
 from concourse.masks import make_identity
 
-U, D, C, I, P = 1024, 512, 1024, 2048, 512
-FLOPS = 2 * U * I * (D + C) + 2 * U * I * P
+USERS, EMB, CONTENT, ITEMS, CELLS = 1024, 512, 1024, 2048, 512
+FLOPS = 2 * USERS * ITEMS * (EMB + CONTENT) + 2 * USERS * ITEMS * CELLS
 
 F32 = mybir.dt.float32
 BF16 = mybir.dt.bfloat16
@@ -19,7 +19,18 @@ ACT = mybir.ActivationFunctionType
 PARTS = 128
 PACK = 4
 SPAN = 512
+PASS_WORDS = SPAN // 2
+BLOCK = 2 * PARTS
 BANKS = 8
+GROUPS = ITEMS // SPAN
+CONTENT_PASSES = CONTENT // SPAN
+TILES = USERS // PARTS
+QUADRANTS = 4
+RUN = 4
+
+PACKED_BUFS = 5
+H_ROWS_BUFS = 4
+EPILOGUE_BUFS = 4
 
 
 def tile_popularity_gated_slate_exposure_k6_kernel(
@@ -27,125 +38,96 @@ def tile_popularity_gated_slate_exposure_k6_kernel(
     mix_words, mix_scales, cell_bias, cell_gain, user_gate, out_0, out_1, out_2,
 ):
     nc = tc.nc
+    on_scalar, on_vector = nc.scalar.copy, nc.vector.tensor_copy
+
     with ExitStack() as ctx:
         keep = ctx.enter_context(tc.tile_pool(name="keep", bufs=1))
         stage = ctx.enter_context(tc.tile_pool(name="stage", bufs=3))
         psum = ctx.enter_context(tc.psum_pool(name="psum", bufs=1))
         ctx.enter_context(tc.manual_schedule())
 
-        banks_used = []
+        banks_taken = []
 
         def next_bank(dtype=F32, width=SPAN):
-            name = "bank%d" % (len(banks_used) % BANKS)
-            banks_used.append(name)
+            name = "bank%d" % (len(banks_taken) % BANKS)
+            banks_taken.append(name)
             return psum.tile([PARTS, width], dtype, name=name)
 
         def kept(name, shape, dtype):
             return keep.tile(shape, dtype, name=name, align_bytes=64)
 
-        ue_raw = [kept("ue_raw%d" % b, [PARTS, 2, D], BF16) for b in range(4)]
-        uc_raw = [kept("uc_raw%d" % b, [PARTS, 2, C], BF16) for b in range(4)]
-        ie_raw = [kept("ie_raw%d" % g, [PARTS, PACK, D], BF16) for g in range(4)]
-        b_words_raw = [kept("b_words_raw%d" % g, [PARTS, 2, 2 * SPAN], U8) for g in range(4)]
-        b_scales_raw = kept("b_scales_raw", [PARTS, 2, I], U8)
-        b_words = [kept("b_words%d" % g, [PARTS, 2, PACK, 2 * PARTS], U8) for g in range(4)]
-        b_scales = [kept("b_scales%d" % g, [PARTS, 2, PACK, PARTS], U8) for g in range(4)]
-        x_words_raw = kept("x_words_raw", [PARTS, 4, P], U32)
-        x_scales_raw = kept("x_scales_raw", [PARTS, P], U8)
-        x_words = kept("x_words", [PARTS, 4, P], U32)
-        x_scales = kept("x_scales", [PARTS, P], U8)
-        ref_raw = kept("ref_raw", [PARTS, 4, PACK], BF16)
-        pop_raw = kept("pop_raw", [PARTS, 4, PACK], BF16)
-        pop = kept("pop", [PARTS, 4, PACK], F32)
-        neg_ref_pop = kept("neg_ref_pop", [PARTS, 4, PACK], F32)
-        bias_raw = kept("bias_raw", [PARTS, PACK], BF16)
-        gain_raw = kept("gain_raw", [PARTS, PACK], BF16)
-        gain = kept("gain", [PARTS, PACK], F32)
-        bias_gain = kept("bias_gain", [PARTS, PACK], F32)
+        ue_raw = [kept("ue_raw%d" % b, [PARTS, 2, EMB], BF16) for b in range(USERS // BLOCK)]
+        uc_raw = [kept("uc_raw%d" % b, [PARTS, 2, CONTENT], BF16) for b in range(USERS // BLOCK)]
+        ie_raw = [kept("ie_raw%d" % g, [PARTS, PACK, EMB], BF16) for g in range(GROUPS)]
+        b_words_raw = [kept("b_words_raw%d" % g, [PARTS, CONTENT_PASSES, 2 * SPAN], U8) for g in range(GROUPS)]
+        b_scales_raw = [
+            kept("b_scales_raw0", [PARTS, CONTENT_PASSES, SPAN], U8),
+            kept("b_scales_raw1", [PARTS, CONTENT_PASSES, ITEMS - SPAN], U8),
+        ]
+        b_words = [kept("b_words%d" % g, [PARTS, CONTENT_PASSES, PACK, 2 * PARTS], U8) for g in range(GROUPS)]
+        b_scales = [kept("b_scales%d" % g, [PARTS, CONTENT_PASSES, PACK, PARTS], U8) for g in range(GROUPS)]
+        x_words = kept("x_words", [PARTS, GROUPS, CELLS], U32)
+        x_scales = kept("x_scales", [PARTS, CELLS], U8)
+        ref_raw = kept("ref_raw", [PARTS, GROUPS, PACK], BF16)
+        pop_raw = kept("pop_raw", [PARTS, GROUPS, PACK], BF16)
+        pop = kept("pop", [PARTS, GROUPS, PACK], F32)
+        neg_ref_pop = kept("neg_ref_pop", [PARTS, GROUPS, PACK], F32)
+        bias_wide = kept("bias_wide", [PARTS, CELLS], BF16)
+        gain_wide = kept("gain_wide", [PARTS, CELLS], BF16)
         gate_rows = kept("gate_rows", [PARTS, PARTS], BF16)
-        gate_cols = kept("gate_cols", [PARTS, 8], F32)
-        gate_wide = kept("gate_wide", [PARTS, U], BF16)
+        gate_cols = kept("gate_cols", [PARTS, TILES], F32)
         ident = kept("ident", [PARTS, PARTS], F32)
         ident_bf = kept("ident_bf", [PARTS, PARTS], BF16)
-        y_codes = kept("y_codes", [PARTS, U], U32)
-        y_scales = kept("y_scales", [PARTS, U], U8)
-        quantised = {}
-        grouped = {}
-        h_rows = {}
-        w_rows = {}
-        z_banks = {}
+        y_codes = kept("y_codes", [PARTS, USERS], U32)
+        y_scales = kept("y_scales", [PARTS, USERS], U8)
+
+        turned, packed, quantised = {}, {}, {}
+        s_banks, h_rows = {}, {}
+        z_banks, biased, y_rows, y_bf, y_packed = {}, {}, {}, {}, {}
 
         def load_users(src, dst, b):
-            nc.sync.dma_start(out=dst[b][:], in_=src[256 * b : 256 * b + 256, :].rearrange("(p j) k -> p j k", j=2))
+            nc.sync.dma_start(out=dst[b][:], in_=src[BLOCK * b : BLOCK * (b + 1), :].rearrange("(j p) k -> p j k", j=2))
 
         def load_items(g):
-            nc.sync.dma_start(out=ie_raw[g][:], in_=item_emb[SPAN * g : SPAN * (g + 1), :].rearrange("(m t) k -> m t k", t=PACK))
+            rows = item_emb[SPAN * g : SPAN * (g + 1), :]
+            nc.sync.dma_start(out=ie_raw[g][:], in_=rows.rearrange("(m t) k -> m t k", t=PACK))
 
         def load_b_words(g):
             src = item_content_words[:, :, 2 * SPAN * g : 2 * SPAN * (g + 1)].rearrange("c p n -> p c n")
             nc.sync.dma_start(out=b_words_raw[g][:].bitcast(I32), in_=src.bitcast(I32))
 
-        nc.vector.memset(b_scales_raw[:].bitcast(I32), 0)
-        nc.vector.memset(x_scales_raw[:].bitcast(I32), 0)
-        make_identity(nc, ident[:])
-        nc.gpsimd.memset(gate_rows[:], 0.0)
-        make_identity(nc, ident_bf[:])
+        def load_b_scales(dst, first, last):
+            for q in range(QUADRANTS):
+                src = item_content_scales[:, 4 * q : 4 * q + 4, first:last].rearrange("c r n -> r c n")
+                nc.sync.dma_start(out=dst[32 * q : 32 * q + 4, :, :].bitcast(I32), in_=src.bitcast(I32))
 
-        load_users(user_emb, ue_raw, 0)
-        load_users(user_emb, ue_raw, 1)
-        load_items(0)
-        load_b_words(0)
-        load_users(user_content, uc_raw, 0)
-        load_users(user_content, uc_raw, 1)
-        for q in range(4):
-            src = item_content_scales[:, 4 * q : 4 * q + 4, :].rearrange("c r n -> r c n")
-            nc.sync.dma_start(out=b_scales_raw[32 * q : 32 * q + 4, :, :].bitcast(I32), in_=src.bitcast(I32))
-        nc.sync.dma_start(out=ref_raw[:], in_=ref_score.rearrange("(g p t) -> p g t", g=4, t=PACK))
-        nc.sync.dma_start(out=pop_raw[:], in_=pop_gate.rearrange("(g p t) -> p g t", g=4, t=PACK))
-        for g in range(1, 4):
-            load_items(g)
-            load_b_words(g)
-        for b in (2, 3):
-            load_users(user_emb, ue_raw, b)
-        for b in (2, 3):
-            load_users(user_content, uc_raw, b)
-        nc.sync.dma_start(out=x_words_raw[:].bitcast(I32), in_=mix_words.rearrange("g p n t -> p g (n t)").bitcast(I32))
-        for q in range(4):
-            nc.sync.dma_start(
-                out=x_scales_raw[32 * q : 32 * q + 16, :].bitcast(I32),
-                in_=mix_scales[:, 4 * q : 4 * q + 4, :].bitcast(I32),
-            )
-        nc.sync.dma_start(out=bias_raw[:], in_=cell_bias.rearrange("(p t) -> p t", t=PACK))
-        nc.sync.dma_start(out=gain_raw[:], in_=cell_gain.rearrange("(p t) -> p t", t=PACK))
-        nc.sync.dma_start(out=gate_rows[0:8, :], in_=user_gate.rearrange("(j p) -> j p", p=PARTS))
-        nc.sync.dma_start(out=gate_wide[:], in_=user_gate.partition_broadcast(PARTS))
+        def words_of(key, part):
+            if key[0] == "ie":
+                return ie_raw[key[1]][:].bitcast(F32)[:, 2 * part : 2 * part + 2, :]
+            if key[0] == "ue":
+                return ue_raw[2 * key[1] + part][:].bitcast(F32)
+            return uc_raw[2 * key[1] + part][:].bitcast(F32)[:, :, PASS_WORDS * key[2] : PASS_WORDS * (key[2] + 1)]
 
-        def copy_on(engine, out, in_):
-            if engine == "scalar":
-                nc.scalar.copy(out=out, in_=in_)
-            else:
-                nc.vector.tensor_copy(out=out, in_=in_)
+        def turn(key, part):
+            turned[key, part] = next_bank()
+            for u in range(2):
+                for j in range(2):
+                    cols = slice((2 * u + j) * PARTS, (2 * u + j + 1) * PARTS)
+                    nc.tensor.transpose(turned[key, part][:, cols], words_of(key, part)[:, j, u:PASS_WORDS:2], ident[:])
 
-        def turn(key, part, engine):
-            kind = key[0]
-            if kind == "ie":
-                words, rows, first = ie_raw[key[1]][:].bitcast(F32), (2 * part, 2 * part + 1), 0
-            elif kind == "ue":
-                words, rows, first = ue_raw[2 * key[1] + part][:].bitcast(F32), (0, 1), 0
-            else:
-                words, rows, first = uc_raw[2 * key[1] + part][:].bitcast(F32), (0, 1), 256 * key[2]
-            bank = next_bank()
-            for j, row in enumerate(rows):
-                for u in range(2):
-                    col = (2 * j + u) * PARTS
-                    nc.tensor.transpose(bank[:, col : col + PARTS], words[:, row, first + u : first + 256 : 2], ident[:])
-            if key not in grouped:
-                grouped[key] = stage.tile([PARTS, PACK * SPAN], BF16, name="grouped", align_bytes=64, bufs=4)
-            dst = grouped[key][:].bitcast(F32)[:, SPAN * part : SPAN * (part + 1)]
-            if kind == "ie":
-                copy_on(engine, dst.rearrange("p (j r u) -> p j r u", j=2, u=2), bank[:].rearrange("p (j u r) -> p j r u", j=2, u=2))
-            else:
-                copy_on(engine, dst.rearrange("p (r j u) -> p r j u", j=2, u=2), bank[:].rearrange("p (j u r) -> p r j u", j=2, u=2))
+        def pack_words(dst, bank):
+            on_scalar(out=dst.rearrange("p (r u) -> p r u", u=2), in_=bank.rearrange("p (u r) -> p r u", u=2))
+
+        def pack(key, part):
+            if part == 0:
+                packed[key] = stage.tile([PARTS, PACK * SPAN], BF16, name="packed", align_bytes=64, bufs=PACKED_BUFS)
+            pack_words(packed[key][:].bitcast(F32)[:, SPAN * part : SPAN * (part + 1)], turned[key, part][:])
+
+        def turn_and_pack(parts):
+            for key, part in parts:
+                turn(key, part)
+            for key, part in parts:
+                pack(key, part)
 
         def quantise(key, first=0, width=SPAN):
             if key not in quantised:
@@ -154,248 +136,264 @@ def tile_popularity_gated_slate_exposure_k6_kernel(
             codes, scales = quantised[key]
             nc.vector.quantize_mx(
                 out=codes[:, first : first + width].bitcast(FP8X4), scales=scales[:, first : first + width],
-                in_=grouped[key][:, PACK * first : PACK * (first + width)],
+                in_=packed[key][:, PACK * first : PACK * (first + width)],
             )
 
         def order_b_words(g):
-            nc.vector.tensor_copy(
+            on_vector(
                 out=b_words[g][:].rearrange("p c t (m b) -> p c t m b", b=2),
                 in_=b_words_raw[g][:].rearrange("p c (m t b) -> p c t m b", t=PACK, b=2),
             )
 
         def order_b_scales(g):
-            nc.vector.tensor_copy(
-                out=b_scales[g][:],
-                in_=b_scales_raw[:, :, SPAN * g : SPAN * (g + 1)].rearrange("p c (m t) -> p c t m", t=PACK),
+            raw = b_scales_raw[1][:, :, SPAN * (g - 1) : SPAN * g] if g else b_scales_raw[0][:]
+            on_vector(out=b_scales[g][:], in_=raw.rearrange("p c (m t) -> p c t m", t=PACK))
+
+        def item_factors():
+            on_vector(out=pop[:], in_=pop_raw[:])
+            nc.vector.scalar_tensor_tensor(
+                out=neg_ref_pop[:], in0=ref_raw[:], scalar=-1.0, in1=pop_raw[:], op0=ALU.mult, op1=ALU.mult
             )
 
-        def order_x():
-            nc.vector.tensor_copy(
-                out=x_words[:].bitcast(I32).rearrange("p g (t c i) -> p g c t i", t=PACK, i=4),
-                in_=x_words_raw[:].bitcast(I32).rearrange("p g (c i t) -> p g c t i", t=PACK, i=4),
-            )
-            nc.vector.tensor_copy(
-                out=x_scales[:].rearrange("p (t m) -> p t m", t=PACK),
-                in_=x_scales_raw[:].rearrange("p (m t) -> p t m", t=PACK),
-            )
-
-        s_banks = {}
-
-        def score_pass(h, g, t, c, start, stop):
-            if start:
+        def score_pass(h, g, t, step):
+            if step == 0:
                 s_banks[h, g, t] = next_bank()
-            cols = slice(PARTS * t, PARTS * (t + 1))
-            if c == "emb":
+                cols = slice(PARTS * t, PARTS * (t + 1))
                 codes, scales = quantised["ie", g]
                 lhs, lhs_scale = codes[:, cols].bitcast(FP8X4), scales[:, cols]
                 rhs, rhs_scale = quantised["ue", h]
             else:
+                c = step - 1
                 lhs, lhs_scale = b_words[g][:, c, t, :].bitcast(FP4X4), b_scales[g][:, c, t, :]
                 rhs, rhs_scale = quantised["uc", h, c]
             nc.tensor.matmul_mx(
-                out=s_banks[h, g, t][:], lhsT=lhs, lhsT_scale=lhs_scale,
-                rhs=rhs[:].bitcast(FP8X4), rhs_scale=rhs_scale[:], start=start, stop=stop,
+                out=s_banks[h, g, t][:], lhsT=lhs, lhsT_scale=lhs_scale, rhs=rhs[:].bitcast(FP8X4),
+                rhs_scale=rhs_scale[:], start=(step == 0), stop=(step == CONTENT_PASSES),
             )
 
         def gate_scores(h, g, t):
             if t == 0:
-                h_rows[h, g] = stage.tile([PARTS, PACK, SPAN], BF16, name="h_rows", align_bytes=64)
+                h_rows[h, g] = stage.tile([PARTS, PACK, SPAN], BF16, name="h_rows", align_bytes=64, bufs=H_ROWS_BUFS)
             nc.scalar.activation(
                 out=h_rows[h, g][:, t, :], in_=s_banks[h, g, t][:], func=ACT.Identity,
                 bias=neg_ref_pop[:, g, t : t + 1], scale=pop[:, g, t : t + 1],
             )
 
-        def scores(h, g):
-            for t in range(PACK):
-                score_pass(h, g, t, "emb", True, False)
-                score_pass(h, g, t, 0, False, False)
-                score_pass(h, g, t, 1, False, True)
+        def scores(h, g, slots=range(PACK)):
+            for t in slots:
+                for step in range(CONTENT_PASSES + 1):
+                    score_pass(h, g, t, step)
                 gate_scores(h, g, t)
 
-        def interleave_h(h, g, engine="vector", first=0, width=SPAN):
+        def pack_h(h, g, copy=on_vector, first=0, width=SPAN):
             if first == 0:
-                grouped["h", h, g] = stage.tile([PARTS, PACK * SPAN], BF16, name="grouped", align_bytes=64, bufs=4)
-            copy_on(
-                engine,
-                grouped["h", h, g][:, PACK * first : PACK * (first + width)].rearrange("p (c i t) -> p c t i", t=PACK, i=4),
-                h_rows[h, g][:, :, first : first + width].rearrange("p t (c i) -> p c t i", i=4),
+                packed["h", h, g] = stage.tile([PARTS, PACK * SPAN], BF16, name="packed", align_bytes=64, bufs=PACKED_BUFS)
+            copy(
+                out=packed["h", h, g][:, PACK * first : PACK * (first + width)].rearrange("p (c i t) -> p c t i", t=PACK, i=RUN),
+                in_=h_rows[h, g][:, :, first : first + width].rearrange("p t (c i) -> p c t i", i=RUN),
             )
 
-        def mix_pass(first, width, t, g):
-            if g == 0:
-                z_banks[first, t] = next_bank(F32, width)
-            cols = slice(PARTS * t, PARTS * (t + 1))
-            codes, scales = quantised["h", first // SPAN, g]
-            users = slice(first % SPAN, first % SPAN + width)
-            nc.tensor.matmul_mx(
-                out=z_banks[first, t][:], lhsT=x_words[:, g, cols].bitcast(FP8X4), lhsT_scale=x_scales[4 * g : PARTS, cols],
-                rhs=codes[:, users].bitcast(FP8X4), rhs_scale=scales[:, users], start=(g == 0), stop=(g == 3),
+        def mix_passes(j, groups):
+            h, users = j // 4, slice(PARTS * (j % 4), PARTS * (j % 4 + 1))
+            for g in groups:
+                if g == 0:
+                    z_banks[j] = next_bank()
+                codes, scales = quantised["h", h, g]
+                nc.tensor.matmul_mx(
+                    out=z_banks[j][:], lhsT=codes[:, users].bitcast(FP8X4), lhsT_scale=scales[:, users],
+                    rhs=x_words[:, g, :].bitcast(FP8X4), rhs_scale=x_scales[4 * g : PARTS, :],
+                    start=(g == 0), stop=(g == GROUPS - 1),
+                )
+
+        def add_bias(j):
+            biased[j] = stage.tile([PARTS, CELLS], F32, name="biased", bufs=EPILOGUE_BUFS)
+            nc.vector.tensor_tensor(out=biased[j][:], in0=z_banks[j][:], in1=bias_wide[:], op=ALU.add)
+
+        def apply_gains(j):
+            y_rows[j] = stage.tile([PARTS, CELLS], F32, name="y_rows", bufs=EPILOGUE_BUFS)
+            nc.vector.scalar_tensor_tensor(
+                out=y_rows[j][:], in0=biased[j][:], scalar=gate_cols[:, j : j + 1], in1=gain_wide[:], op0=ALU.mult, op1=ALU.mult
             )
 
-        def scale_on(engine, out, in_, scale, bias):
-            if engine == "scalar":
-                nc.scalar.activation(out=out, in_=in_, func=ACT.Identity, bias=bias, scale=scale)
-            else:
-                nc.vector.tensor_scalar(out=out, in0=in_, scalar1=scale, scalar2=bias, op0=ALU.mult, op1=ALU.add)
+        def store_y(j):
+            nc.sync.dma_start(out=out_0[PARTS * j : PARTS * (j + 1), :], in_=y_rows[j][:])
 
-        def cell_affine(first, width, t, engine):
-            if t == 0:
-                w_rows[first] = kept("w_rows%d" % first, [PARTS, PACK, width], F32)
-            scale_on(engine, w_rows[first][:, t, :], z_banks[first, t][:], gain[:, t : t + 1], bias_gain[:, t : t + 1])
+        def round_y(j, copy):
+            y_bf[j] = stage.tile([PARTS, CELLS], BF16, name="y_bf", bufs=TILES)
+            copy(out=y_bf[j][:], in_=y_rows[j][:])
 
-        def turn_out(first, j, engine="scalar"):
-            bank = next_bank()
-            for t in range(PACK):
-                nc.tensor.transpose(bank[:, PARTS * t : PARTS * (t + 1)], w_rows[first][:, t, PARTS * j : PARTS * (j + 1)], ident[:])
-            y_rows = stage.tile([PARTS, P], F32, name="y_rows", bufs=4)
-            tile_no = first // PARTS + j
-            out = y_rows[:].rearrange("u (p t) -> u p t", t=PACK)
-            in_ = bank[:].rearrange("u (t p) -> u p t", t=PACK)
-            gate = gate_cols[:, tile_no : tile_no + 1]
-            if engine == "scalar":
-                nc.scalar.activation(out=out, in_=in_, func=ACT.Copy, scale=gate)
-            else:
-                nc.vector.tensor_scalar(out=out, in0=in_, scalar1=gate, scalar2=None, op0=ALU.mult)
-            nc.sync.dma_start(out=out_0[PARTS * tile_no : PARTS * (tile_no + 1), :], in_=y_rows[:])
+        def turn_y(j):
+            turned["y", j] = next_bank(F32, 2 * PARTS)
+            for u in range(2):
+                words = y_bf[j][:].bitcast(F32)[:, u:PASS_WORDS:2]
+                nc.tensor.transpose(turned["y", j][:, PARTS * u : PARTS * (u + 1)], words, ident[:])
 
-        def gate_y(first, width):
-            grouped["y", first] = stage.tile([PARTS, PACK * width], BF16, name="y_grouped", align_bytes=64)
-            nc.vector.tensor_tensor(
-                out=grouped["y", first][:].rearrange("p (c i t) -> p c t i", t=PACK, i=4),
-                in0=w_rows[first][:].rearrange("p t (c i) -> p c t i", i=4),
-                in1=gate_wide[:, first : first + width].rearrange("p (c i) -> p c i", i=4).unsqueeze(2).to_broadcast([PARTS, width // 4, PACK, 4]),
-                op=ALU.mult,
+        def pack_y(j):
+            y_packed[j] = stage.tile([PARTS, PACK * PARTS], BF16, name="y_packed", align_bytes=64, bufs=TILES)
+            pack_words(y_packed[j][:].bitcast(F32), turned["y", j][:])
+
+        def quantise_y(j):
+            users = slice(PARTS * j, PARTS * (j + 1))
+            nc.vector.quantize_mx(out=y_codes[:, users].bitcast(FP8X4), scales=y_scales[:, users], in_=y_packed[j][:])
+
+        def store_codes(first_tile, last_tile):
+            users = slice(PARTS * first_tile, PARTS * (last_tile + 1))
+            dst = out_1[0].rearrange("p m t -> p (m t)").bitcast(I32)
+            nc.sync.dma_start(out=dst[:, users], in_=y_codes[:, users].bitcast(I32))
+
+        nc.vector.memset(b_scales_raw[0][:].bitcast(I32), 0)
+        nc.vector.memset(b_scales_raw[1][:].bitcast(I32), 0)
+        nc.vector.memset(x_scales[:].bitcast(I32), 0)
+        make_identity(nc, ident[:])
+        nc.vector.memset(gate_rows[:], 0.0)
+        on_vector(out=ident_bf[:], in_=ident[:])
+
+        load_users(user_emb, ue_raw, 0)
+        load_items(0)
+        load_b_words(0)
+        load_users(user_emb, ue_raw, 1)
+        load_users(user_content, uc_raw, 0)
+        load_users(user_content, uc_raw, 1)
+        load_items(1)
+        load_b_scales(b_scales_raw[0], 0, SPAN)
+        load_items(2)
+        nc.sync.dma_start(out=ref_raw[:], in_=ref_score.rearrange("(g p t) -> p g t", g=GROUPS, t=PACK))
+        nc.sync.dma_start(out=pop_raw[:], in_=pop_gate.rearrange("(g p t) -> p g t", g=GROUPS, t=PACK))
+        load_b_scales(b_scales_raw[1], SPAN, ITEMS)
+        load_b_words(1)
+        load_items(3)
+        load_b_words(2)
+        for src, dst in ((user_emb, ue_raw), (user_content, uc_raw)):
+            load_users(src, dst, 2)
+            load_users(src, dst, 3)
+        load_b_words(3)
+        nc.sync.dma_start(out=x_words[:].bitcast(I32), in_=mix_words.rearrange("g p n t -> p g (n t)").bitcast(I32))
+        for q in range(QUADRANTS):
+            nc.sync.dma_start(
+                out=x_scales[32 * q : 32 * q + 4 * GROUPS, :].bitcast(I32),
+                in_=mix_scales[:, 4 * q : 4 * q + 4, :].bitcast(I32),
             )
+        nc.sync.dma_start(out=gate_rows[0:TILES, :], in_=user_gate.rearrange("(j p) -> j p", p=PARTS))
+        nc.sync.dma_start(out=bias_wide[:], in_=cell_bias.partition_broadcast(PARTS))
+        nc.sync.dma_start(out=gain_wide[:], in_=cell_gain.partition_broadcast(PARTS))
 
-        def quantise_y(first, width):
-            cols = slice(first, first + width)
-            nc.vector.quantize_mx(out=y_codes[:, cols].bitcast(FP8X4), scales=y_scales[:, cols], in_=grouped["y", first][:])
-
-        def store_codes(first, width):
-            cols = slice(first, first + width)
-            nc.sync.dma_start(out=out_1[0].rearrange("p m t -> p (m t)").bitcast(I32)[:, cols], in_=y_codes[:, cols].bitcast(I32))
-
-        def store_scales():
-            for q in range(4):
-                nc.sync.dma_start(out=out_2[0, 4 * q : 4 * q + 4, :].bitcast(I32), in_=y_scales[32 * q : 32 * q + 4, :].bitcast(I32))
-
-        def item_constants():
-            nc.vector.tensor_copy(out=pop[:], in_=pop_raw[:])
-            nc.vector.scalar_tensor_tensor(out=neg_ref_pop[:], in0=ref_raw[:], scalar=-1.0, in1=pop_raw[:], op0=ALU.mult, op1=ALU.mult)
-
-        def cell_constants():
-            nc.vector.tensor_copy(out=gain[:], in_=gain_raw[:])
-            nc.vector.tensor_tensor(out=bias_gain[:], in0=bias_raw[:], in1=gain_raw[:], op=ALU.mult)
-
-        def user_constants():
-            bank = next_bank(BF16, PARTS)
-            nc.tensor.transpose(bank[:], gate_rows[:], ident_bf[:])
-            nc.vector.tensor_copy(out=gate_cols[:], in_=bank[:, 0:8])
-
-        turn(("ue", 0), 0, "scalar")
-        turn(("ue", 0), 1, "vector")
-        turn(("ie", 0), 0, "scalar")
-        quantise(("ue", 0))
-        turn(("ie", 0), 1, "scalar")
+        for key, part in ((("ue", 0), 0), (("ie", 0), 0), (("ie", 0), 1), (("ue", 0), 1)):
+            turn_and_pack([(key, part)])
         order_b_words(0)
         quantise(("ie", 0))
-        turn(("uc", 0, 0), 0, "scalar")
-        turn(("uc", 0, 1), 0, "scalar")
-        turn(("uc", 0, 0), 1, "scalar")
-        turn(("uc", 0, 1), 1, "vector")
+        quantise(("ue", 0))
+        turn_and_pack([(("uc", 0, c), part) for part in range(2) for c in range(CONTENT_PASSES)])
         quantise(("uc", 0, 0))
         order_b_scales(0)
         quantise(("uc", 0, 1))
-        item_constants()
-        for t in range(PACK):
-            score_pass(0, 0, t, "emb", True, False)
-        turn(("ie", 1), 0, "scalar")
-        turn(("ie", 1), 1, "scalar")
-        order_b_words(1)
-        quantise(("ie", 1))
+        item_factors()
+        turn_and_pack([(("ie", 1), 0), (("ie", 1), 1)])
+
+        for step in range(CONTENT_PASSES):
+            for t in range(PACK):
+                score_pass(0, 0, t, step)
         order_b_scales(1)
-        for t in range(PACK):
-            score_pass(0, 0, t, 0, False, False)
-            score_pass(0, 0, t, 1, False, True)
-            gate_scores(0, 0, t)
-        turn(("ie", 2), 0, "scalar")
-        turn(("ie", 2), 1, "scalar")
-        interleave_h(0, 0)
-        order_b_words(2)
-        quantise(("ie", 2))
+        quantise(("ie", 1))
+        order_b_words(1)
         order_b_scales(2)
-        quantise(("h", 0, 0))
-        scores(0, 1)
-        turn(("ie", 3), 0, "scalar")
-        turn(("ie", 3), 1, "scalar")
-        turn(("ue", 1), 0, "scalar")
-        turn(("ue", 1), 1, "scalar")
-        order_b_words(3)
-        interleave_h(0, 1)
-        quantise(("ie", 3))
-        order_b_scales(3)
-        quantise(("h", 0, 1))
-        quantise(("ue", 1))
-        scores(0, 2)
-        turn(("uc", 1, 0), 0, "scalar")
-        turn(("uc", 1, 0), 1, "vector")
-        turn(("uc", 1, 1), 0, "scalar")
-        turn(("uc", 1, 1), 1, "vector")
-        interleave_h(0, 2)
-        quantise(("uc", 1, 0))
-        quantise(("uc", 1, 1))
-        quantise(("h", 0, 2))
-        scores(0, 3)
-        interleave_h(0, 3)
-        cell_constants()
-        quantise(("h", 0, 3))
-        scores(1, 0)
-        order_x()
-        interleave_h(1, 0)
-        user_constants()
-        quantise(("h", 1, 0))
-        scores(1, 1)
-        interleave_h(1, 1)
+        order_b_words(2)
         for t in range(PACK):
-            for g in range(4):
-                mix_pass(0, SPAN, t, g)
-            cell_affine(0, SPAN, t, "scalar")
-        quantise(("h", 1, 1))
-        scores(1, 2)
-        gate_y(0, SPAN)
-        interleave_h(1, 2)
-        quantise_y(0, SPAN)
-        store_codes(0, SPAN)
+            score_pass(0, 0, t, CONTENT_PASSES)
+            gate_scores(0, 0, t)
+
+        turn_and_pack([(("ie", g), part) for g in (2, 3) for part in range(2)])
+        quantise(("ie", 2))
+        order_b_scales(3)
+        order_b_words(3)
+        quantise(("ie", 3))
+        scores(0, 1)
+
+        turn_and_pack([(key, part) for key in (("ue", 1), ("uc", 1, 0)) for part in range(2)])
+        pack_h(0, 0)
+        quantise(("ue", 1))
+        quantise(("uc", 1, 0))
+        quantise(("h", 0, 0))
+        pack_h(0, 1)
+        scores(0, 2)
+
+        turn_and_pack([(("uc", 1, 1), 0), (("uc", 1, 1), 1)])
+        gate_bank = next_bank(BF16, PARTS)
+        nc.tensor.transpose(gate_bank[:], gate_rows[:], ident_bf[:])
+        quantise(("h", 0, 1))
+        on_vector(out=gate_cols[:], in_=gate_bank[:, 0:TILES])
+        quantise(("uc", 1, 1))
+        pack_h(0, 2)
+        scores(0, 3)
+
+        quantise(("h", 0, 2))
+        pack_h(0, 3)
+        scores(1, 0)
+        quantise(("h", 0, 3))
+        pack_h(1, 0)
+
+        scores(1, 1, (0, 1))
         for j in range(4):
-            turn_out(0, j)
+            mix_passes(j, range(GROUPS))
+        quantise(("h", 1, 0))
+        for j in range(4):
+            add_bias(j)
+            apply_gains(j)
+        for j in range(4):
+            store_y(j)
+        scores(1, 1, (2, 3))
+        pack_h(1, 1)
+        round_y(0, on_vector)
+        round_y(1, on_vector)
+        quantise(("h", 1, 1))
+        round_y(2, on_vector)
+        round_y(3, on_vector)
+        scores(1, 2)
+        pack_h(1, 2)
         quantise(("h", 1, 2))
         scores(1, 3)
-        interleave_h(1, 3, "vector", 0, 256)
-        interleave_h(1, 3, "scalar", 256, 256)
-        quantise(("h", 1, 3), 0, 256)
-        quantise(("h", 1, 3), 256, 256)
-        for g in range(3):
-            for t in range(PACK):
-                mix_pass(512, 256, t, g)
-        for t in (0, 1):
-            for g in range(3):
-                mix_pass(768, 256, t, g)
-        for t in range(PACK):
-            mix_pass(512, 256, t, 3)
-            cell_affine(512, 256, t, "scalar" if t in (0, 2) else "vector")
-        gate_y(512, 256)
-        for t in (2, 3):
-            for g in range(3):
-                mix_pass(768, 256, t, g)
-        for t in range(PACK):
-            mix_pass(768, 256, t, 3)
-            cell_affine(768, 256, t, "scalar" if t in (0, 1, 2) else "vector")
-        quantise_y(512, 256)
-        turn_out(512, 0, "scalar")
-        turn_out(512, 1, "scalar")
-        gate_y(768, 256)
-        turn_out(768, 0, "scalar")
-        quantise_y(768, 256)
-        store_codes(512, 512)
-        turn_out(768, 1, "scalar")
-        store_scales()
+
+        last_pieces = ((0, PARTS, on_vector), (PARTS, PARTS, on_vector), (BLOCK, BLOCK, on_scalar))
+        for first, width, copy in last_pieces:
+            pack_h(1, 3, copy, first, width)
+        for first, width, copy in last_pieces:
+            quantise(("h", 1, 3), first, width)
+        for pair in ((4, 5), (6, 7)):
+            for j in pair:
+                mix_passes(j, range(GROUPS - 1))
+            for j in pair:
+                mix_passes(j, [GROUPS - 1])
+
+        for action in (add_bias, apply_gains, store_y):
+            action(4)
+            action(5)
+        round_y(4, on_scalar)
+        round_y(5, on_scalar)
+        for j in range(6):
+            turn_y(j)
+        for j in range(4):
+            pack_y(j)
+        for action in (add_bias, apply_gains, store_y):
+            action(6)
+            action(7)
+        round_y(6, on_scalar)
+        quantise_y(0)
+        round_y(7, on_vector)
+        pack_y(4)
+        pack_y(5)
+        turn_y(6)
+        turn_y(7)
+        for j in (1, 2, 3):
+            quantise_y(j)
+        store_codes(0, 3)
+        quantise_y(4)
+        quantise_y(5)
+        store_codes(4, 5)
+        pack_y(6)
+        pack_y(7)
+        quantise_y(6)
+        quantise_y(7)
+        store_codes(6, 7)
+        for q in range(QUADRANTS):
+            nc.sync.dma_start(
+                out=out_2[0, 4 * q : 4 * q + 4, :].bitcast(I32), in_=y_scales[32 * q : 32 * q + 4, :].bitcast(I32)
+            )

from contextlib import ExitStack

import concourse.mybir as mybir
from concourse.masks import make_identity

USERS, EMB, CONTENT, ITEMS, CELLS = 1024, 512, 1024, 2048, 512
FLOPS = 2 * USERS * ITEMS * (EMB + CONTENT) + 2 * USERS * ITEMS * CELLS

F32 = mybir.dt.float32
BF16 = mybir.dt.bfloat16
U32 = mybir.dt.uint32
I32 = mybir.dt.int32
U8 = mybir.dt.uint8
FP8X4 = mybir.dt.float8_e4m3fn_x4
FP4X4 = mybir.dt.float4_e2m1fn_x4
ALU = mybir.AluOpType
ACT = mybir.ActivationFunctionType

PARTS = 128
PACK = 4
SPAN = 512
PASS_WORDS = SPAN // 2
BLOCK = 2 * PARTS
BANKS = 8
GROUPS = ITEMS // SPAN
CONTENT_PASSES = CONTENT // SPAN
TILES = USERS // PARTS
QUADRANTS = 4
RUN = 4

PACKED_BUFS = 5
H_ROWS_BUFS = 4
EPILOGUE_BUFS = 4


def tile_popularity_gated_slate_exposure_k6_kernel(
    tc, user_emb, item_emb, user_content, item_content_words, item_content_scales, ref_score, pop_gate,
    mix_words, mix_scales, cell_bias, cell_gain, user_gate, out_0, out_1, out_2,
):
    nc = tc.nc
    on_scalar, on_vector = nc.scalar.copy, nc.vector.tensor_copy

    with ExitStack() as ctx:
        keep = ctx.enter_context(tc.tile_pool(name="keep", bufs=1))
        stage = ctx.enter_context(tc.tile_pool(name="stage", bufs=3))
        psum = ctx.enter_context(tc.psum_pool(name="psum", bufs=1))
        ctx.enter_context(tc.manual_schedule())

        banks_taken = []

        def next_bank(dtype=F32, width=SPAN):
            name = "bank%d" % (len(banks_taken) % BANKS)
            banks_taken.append(name)
            return psum.tile([PARTS, width], dtype, name=name)

        def kept(name, shape, dtype):
            return keep.tile(shape, dtype, name=name, align_bytes=64)

        ue_raw = [kept("ue_raw%d" % b, [PARTS, 2, EMB], BF16) for b in range(USERS // BLOCK)]
        uc_raw = [kept("uc_raw%d" % b, [PARTS, 2, CONTENT], BF16) for b in range(USERS // BLOCK)]
        ie_raw = [kept("ie_raw%d" % g, [PARTS, PACK, EMB], BF16) for g in range(GROUPS)]
        b_words_raw = [kept("b_words_raw%d" % g, [PARTS, CONTENT_PASSES, 2 * SPAN], U8) for g in range(GROUPS)]
        b_scales_raw = [
            kept("b_scales_raw0", [PARTS, CONTENT_PASSES, SPAN], U8),
            kept("b_scales_raw1", [PARTS, CONTENT_PASSES, ITEMS - SPAN], U8),
        ]
        b_words = [kept("b_words%d" % g, [PARTS, CONTENT_PASSES, PACK, 2 * PARTS], U8) for g in range(GROUPS)]
        b_scales = [kept("b_scales%d" % g, [PARTS, CONTENT_PASSES, PACK, PARTS], U8) for g in range(GROUPS)]
        x_words = kept("x_words", [PARTS, GROUPS, CELLS], U32)
        x_scales = kept("x_scales", [PARTS, CELLS], U8)
        ref_raw = kept("ref_raw", [PARTS, GROUPS, PACK], BF16)
        pop_raw = kept("pop_raw", [PARTS, GROUPS, PACK], BF16)
        pop = kept("pop", [PARTS, GROUPS, PACK], F32)
        neg_ref_pop = kept("neg_ref_pop", [PARTS, GROUPS, PACK], F32)
        bias_wide = kept("bias_wide", [PARTS, CELLS], BF16)
        gain_wide = kept("gain_wide", [PARTS, CELLS], BF16)
        gate_rows = kept("gate_rows", [PARTS, PARTS], BF16)
        gate_cols = kept("gate_cols", [PARTS, TILES], F32)
        ident = kept("ident", [PARTS, PARTS], F32)
        ident_bf = kept("ident_bf", [PARTS, PARTS], BF16)
        y_codes = kept("y_codes", [PARTS, USERS], U32)
        y_scales = kept("y_scales", [PARTS, USERS], U8)

        turned, packed, quantised = {}, {}, {}
        s_banks, h_rows = {}, {}
        z_banks, biased, y_rows, y_bf, y_packed = {}, {}, {}, {}, {}

        def load_users(src, dst, b):
            nc.sync.dma_start(out=dst[b][:], in_=src[BLOCK * b : BLOCK * (b + 1), :].rearrange("(j p) k -> p j k", j=2))

        def load_items(g):
            rows = item_emb[SPAN * g : SPAN * (g + 1), :]
            nc.sync.dma_start(out=ie_raw[g][:], in_=rows.rearrange("(m t) k -> m t k", t=PACK))

        def load_b_words(g):
            src = item_content_words[:, :, 2 * SPAN * g : 2 * SPAN * (g + 1)].rearrange("c p n -> p c n")
            nc.sync.dma_start(out=b_words_raw[g][:].bitcast(I32), in_=src.bitcast(I32))

        def load_b_scales(dst, first, last):
            for q in range(QUADRANTS):
                src = item_content_scales[:, 4 * q : 4 * q + 4, first:last].rearrange("c r n -> r c n")
                nc.sync.dma_start(out=dst[32 * q : 32 * q + 4, :, :].bitcast(I32), in_=src.bitcast(I32))

        def words_of(key, part):
            if key[0] == "ie":
                return ie_raw[key[1]][:].bitcast(F32)[:, 2 * part : 2 * part + 2, :]
            if key[0] == "ue":
                return ue_raw[2 * key[1] + part][:].bitcast(F32)
            return uc_raw[2 * key[1] + part][:].bitcast(F32)[:, :, PASS_WORDS * key[2] : PASS_WORDS * (key[2] + 1)]

        def turn(key, part):
            turned[key, part] = next_bank()
            for u in range(2):
                for j in range(2):
                    cols = slice((2 * u + j) * PARTS, (2 * u + j + 1) * PARTS)
                    nc.tensor.transpose(turned[key, part][:, cols], words_of(key, part)[:, j, u:PASS_WORDS:2], ident[:])

        def pack_words(dst, bank):
            on_scalar(out=dst.rearrange("p (r u) -> p r u", u=2), in_=bank.rearrange("p (u r) -> p r u", u=2))

        def pack(key, part):
            if part == 0:
                packed[key] = stage.tile([PARTS, PACK * SPAN], BF16, name="packed", align_bytes=64, bufs=PACKED_BUFS)
            pack_words(packed[key][:].bitcast(F32)[:, SPAN * part : SPAN * (part + 1)], turned[key, part][:])

        def turn_and_pack(parts):
            for key, part in parts:
                turn(key, part)
            for key, part in parts:
                pack(key, part)

        def quantise(key, first=0, width=SPAN):
            if key not in quantised:
                name = "_".join(str(k) for k in key)
                quantised[key] = (kept("codes_" + name, [PARTS, SPAN], U32), kept("scales_" + name, [PARTS, SPAN], U8))
            codes, scales = quantised[key]
            nc.vector.quantize_mx(
                out=codes[:, first : first + width].bitcast(FP8X4), scales=scales[:, first : first + width],
                in_=packed[key][:, PACK * first : PACK * (first + width)],
            )

        def order_b_words(g):
            on_vector(
                out=b_words[g][:].rearrange("p c t (m b) -> p c t m b", b=2),
                in_=b_words_raw[g][:].rearrange("p c (m t b) -> p c t m b", t=PACK, b=2),
            )

        def order_b_scales(g):
            raw = b_scales_raw[1][:, :, SPAN * (g - 1) : SPAN * g] if g else b_scales_raw[0][:]
            on_vector(out=b_scales[g][:], in_=raw.rearrange("p c (m t) -> p c t m", t=PACK))

        def item_factors():
            on_vector(out=pop[:], in_=pop_raw[:])
            nc.vector.scalar_tensor_tensor(
                out=neg_ref_pop[:], in0=ref_raw[:], scalar=-1.0, in1=pop_raw[:], op0=ALU.mult, op1=ALU.mult
            )

        def score_pass(h, g, t, step):
            if step == 0:
                s_banks[h, g, t] = next_bank()
                cols = slice(PARTS * t, PARTS * (t + 1))
                codes, scales = quantised["ie", g]
                lhs, lhs_scale = codes[:, cols].bitcast(FP8X4), scales[:, cols]
                rhs, rhs_scale = quantised["ue", h]
            else:
                c = step - 1
                lhs, lhs_scale = b_words[g][:, c, t, :].bitcast(FP4X4), b_scales[g][:, c, t, :]
                rhs, rhs_scale = quantised["uc", h, c]
            nc.tensor.matmul_mx(
                out=s_banks[h, g, t][:], lhsT=lhs, lhsT_scale=lhs_scale, rhs=rhs[:].bitcast(FP8X4),
                rhs_scale=rhs_scale[:], start=(step == 0), stop=(step == CONTENT_PASSES),
            )

        def gate_scores(h, g, t):
            if t == 0:
                h_rows[h, g] = stage.tile([PARTS, PACK, SPAN], BF16, name="h_rows", align_bytes=64, bufs=H_ROWS_BUFS)
            nc.scalar.activation(
                out=h_rows[h, g][:, t, :], in_=s_banks[h, g, t][:], func=ACT.Identity,
                bias=neg_ref_pop[:, g, t : t + 1], scale=pop[:, g, t : t + 1],
            )

        def scores(h, g, slots=range(PACK)):
            for t in slots:
                for step in range(CONTENT_PASSES + 1):
                    score_pass(h, g, t, step)
                gate_scores(h, g, t)

        def pack_h(h, g, copy=on_vector, first=0, width=SPAN):
            if first == 0:
                packed["h", h, g] = stage.tile([PARTS, PACK * SPAN], BF16, name="packed", align_bytes=64, bufs=PACKED_BUFS)
            copy(
                out=packed["h", h, g][:, PACK * first : PACK * (first + width)].rearrange("p (c i t) -> p c t i", t=PACK, i=RUN),
                in_=h_rows[h, g][:, :, first : first + width].rearrange("p t (c i) -> p c t i", i=RUN),
            )

        def mix_passes(j, groups):
            h, users = j // 4, slice(PARTS * (j % 4), PARTS * (j % 4 + 1))
            for g in groups:
                if g == 0:
                    z_banks[j] = next_bank()
                codes, scales = quantised["h", h, g]
                nc.tensor.matmul_mx(
                    out=z_banks[j][:], lhsT=codes[:, users].bitcast(FP8X4), lhsT_scale=scales[:, users],
                    rhs=x_words[:, g, :].bitcast(FP8X4), rhs_scale=x_scales[4 * g : PARTS, :],
                    start=(g == 0), stop=(g == GROUPS - 1),
                )

        def add_bias(j):
            biased[j] = stage.tile([PARTS, CELLS], F32, name="biased", bufs=EPILOGUE_BUFS)
            nc.vector.tensor_tensor(out=biased[j][:], in0=z_banks[j][:], in1=bias_wide[:], op=ALU.add)

        def apply_gains(j):
            y_rows[j] = stage.tile([PARTS, CELLS], F32, name="y_rows", bufs=EPILOGUE_BUFS)
            nc.vector.scalar_tensor_tensor(
                out=y_rows[j][:], in0=biased[j][:], scalar=gate_cols[:, j : j + 1], in1=gain_wide[:], op0=ALU.mult, op1=ALU.mult
            )

        def store_y(j):
            nc.sync.dma_start(out=out_0[PARTS * j : PARTS * (j + 1), :], in_=y_rows[j][:])

        def round_y(j, copy):
            y_bf[j] = stage.tile([PARTS, CELLS], BF16, name="y_bf", bufs=TILES)
            copy(out=y_bf[j][:], in_=y_rows[j][:])

        def turn_y(j):
            turned["y", j] = next_bank(F32, 2 * PARTS)
            for u in range(2):
                words = y_bf[j][:].bitcast(F32)[:, u:PASS_WORDS:2]
                nc.tensor.transpose(turned["y", j][:, PARTS * u : PARTS * (u + 1)], words, ident[:])

        def pack_y(j):
            y_packed[j] = stage.tile([PARTS, PACK * PARTS], BF16, name="y_packed", align_bytes=64, bufs=TILES)
            pack_words(y_packed[j][:].bitcast(F32), turned["y", j][:])

        def quantise_y(j):
            users = slice(PARTS * j, PARTS * (j + 1))
            nc.vector.quantize_mx(out=y_codes[:, users].bitcast(FP8X4), scales=y_scales[:, users], in_=y_packed[j][:])

        def store_codes(first_tile, last_tile):
            users = slice(PARTS * first_tile, PARTS * (last_tile + 1))
            dst = out_1[0].rearrange("p m t -> p (m t)").bitcast(I32)
            nc.sync.dma_start(out=dst[:, users], in_=y_codes[:, users].bitcast(I32))

        nc.vector.memset(b_scales_raw[0][:].bitcast(I32), 0)
        nc.vector.memset(b_scales_raw[1][:].bitcast(I32), 0)
        nc.vector.memset(x_scales[:].bitcast(I32), 0)
        make_identity(nc, ident[:])
        nc.vector.memset(gate_rows[:], 0.0)
        on_vector(out=ident_bf[:], in_=ident[:])

        load_users(user_emb, ue_raw, 0)
        load_items(0)
        load_b_words(0)
        load_users(user_emb, ue_raw, 1)
        load_users(user_content, uc_raw, 0)
        load_users(user_content, uc_raw, 1)
        load_items(1)
        load_b_scales(b_scales_raw[0], 0, SPAN)
        load_items(2)
        nc.sync.dma_start(out=ref_raw[:], in_=ref_score.rearrange("(g p t) -> p g t", g=GROUPS, t=PACK))
        nc.sync.dma_start(out=pop_raw[:], in_=pop_gate.rearrange("(g p t) -> p g t", g=GROUPS, t=PACK))
        load_b_scales(b_scales_raw[1], SPAN, ITEMS)
        load_b_words(1)
        load_items(3)
        load_b_words(2)
        for src, dst in ((user_emb, ue_raw), (user_content, uc_raw)):
            load_users(src, dst, 2)
            load_users(src, dst, 3)
        load_b_words(3)
        nc.sync.dma_start(out=x_words[:].bitcast(I32), in_=mix_words.rearrange("g p n t -> p g (n t)").bitcast(I32))
        for q in range(QUADRANTS):
            nc.sync.dma_start(
                out=x_scales[32 * q : 32 * q + 4 * GROUPS, :].bitcast(I32),
                in_=mix_scales[:, 4 * q : 4 * q + 4, :].bitcast(I32),
            )
        nc.sync.dma_start(out=gate_rows[0:TILES, :], in_=user_gate.rearrange("(j p) -> j p", p=PARTS))
        nc.sync.dma_start(out=bias_wide[:], in_=cell_bias.partition_broadcast(PARTS))
        nc.sync.dma_start(out=gain_wide[:], in_=cell_gain.partition_broadcast(PARTS))

        for key, part in ((("ue", 0), 0), (("ie", 0), 0), (("ie", 0), 1), (("ue", 0), 1)):
            turn_and_pack([(key, part)])
        order_b_words(0)
        quantise(("ie", 0))
        quantise(("ue", 0))
        turn_and_pack([(("uc", 0, c), part) for part in range(2) for c in range(CONTENT_PASSES)])
        quantise(("uc", 0, 0))
        order_b_scales(0)
        quantise(("uc", 0, 1))
        item_factors()
        turn_and_pack([(("ie", 1), 0), (("ie", 1), 1)])

        for step in range(CONTENT_PASSES):
            for t in range(PACK):
                score_pass(0, 0, t, step)
        order_b_scales(1)
        quantise(("ie", 1))
        order_b_words(1)
        order_b_scales(2)
        order_b_words(2)
        for t in range(PACK):
            score_pass(0, 0, t, CONTENT_PASSES)
            gate_scores(0, 0, t)

        turn_and_pack([(("ie", g), part) for g in (2, 3) for part in range(2)])
        quantise(("ie", 2))
        order_b_scales(3)
        order_b_words(3)
        quantise(("ie", 3))
        scores(0, 1)

        turn_and_pack([(key, part) for key in (("ue", 1), ("uc", 1, 0)) for part in range(2)])
        pack_h(0, 0)
        quantise(("ue", 1))
        quantise(("uc", 1, 0))
        quantise(("h", 0, 0))
        pack_h(0, 1)
        scores(0, 2)

        turn_and_pack([(("uc", 1, 1), 0), (("uc", 1, 1), 1)])
        gate_bank = next_bank(BF16, PARTS)
        nc.tensor.transpose(gate_bank[:], gate_rows[:], ident_bf[:])
        quantise(("h", 0, 1))
        on_vector(out=gate_cols[:], in_=gate_bank[:, 0:TILES])
        quantise(("uc", 1, 1))
        pack_h(0, 2)
        scores(0, 3)

        quantise(("h", 0, 2))
        pack_h(0, 3)
        scores(1, 0)
        quantise(("h", 0, 3))
        pack_h(1, 0)

        scores(1, 1, (0, 1))
        for j in range(4):
            mix_passes(j, range(GROUPS))
        quantise(("h", 1, 0))
        for j in range(4):
            add_bias(j)
            apply_gains(j)
        for j in range(4):
            store_y(j)
        scores(1, 1, (2, 3))
        pack_h(1, 1)
        round_y(0, on_vector)
        round_y(1, on_vector)
        quantise(("h", 1, 1))
        round_y(2, on_vector)
        round_y(3, on_vector)
        scores(1, 2)
        pack_h(1, 2)
        quantise(("h", 1, 2))
        scores(1, 3)

        last_pieces = ((0, PARTS, on_vector), (PARTS, PARTS, on_vector), (BLOCK, BLOCK, on_scalar))
        for first, width, copy in last_pieces:
            pack_h(1, 3, copy, first, width)
        for first, width, copy in last_pieces:
            quantise(("h", 1, 3), first, width)
        for pair in ((4, 5), (6, 7)):
            for j in pair:
                mix_passes(j, range(GROUPS - 1))
            for j in pair:
                mix_passes(j, [GROUPS - 1])

        for action in (add_bias, apply_gains, store_y):
            action(4)
            action(5)
        round_y(4, on_scalar)
        round_y(5, on_scalar)
        for j in range(6):
            turn_y(j)
        for j in range(4):
            pack_y(j)
        for action in (add_bias, apply_gains, store_y):
            action(6)
            action(7)
        round_y(6, on_scalar)
        quantise_y(0)
        round_y(7, on_vector)
        pack_y(4)
        pack_y(5)
        turn_y(6)
        turn_y(7)
        for j in (1, 2, 3):
            quantise_y(j)
        store_codes(0, 3)
        quantise_y(4)
        quantise_y(5)
        store_codes(4, 5)
        pack_y(6)
        pack_y(7)
        quantise_y(6)
        quantise_y(7)
        store_codes(6, 7)
        for q in range(QUADRANTS):
            nc.sync.dma_start(
                out=out_2[0, 4 * q : 4 * q + 4, :].bitcast(I32), in_=y_scales[32 * q : 32 * q + 4, :].bitcast(I32)
            )
